import numpy as np
import ml_dtypes


def mxq(x, axis, fmt="e4m3"):
    dtype, down = {"e4m3": (ml_dtypes.float8_e4m3fn, 7), "e5m2": (ml_dtypes.float8_e5m2, 14)}[fmt]
    v = np.moveaxis(np.asarray(x, np.float32).astype(ml_dtypes.bfloat16).astype(np.float64), axis, -1)
    blocks = v.reshape(v.shape[:-1] + (-1, 32))
    amax = np.abs(blocks).max(-1, keepdims=True)
    byte = np.maximum(np.where(amax > 0, np.frexp(amax)[1] - 1 + 127, 0) - down, 1)
    scale = np.exp2(byte - 127.0)
    codes = (blocks / scale).astype(np.float32).astype(dtype).astype(np.float64)
    return np.moveaxis((codes * scale).reshape(v.shape), -1, axis)


WIDE = False


def mx_kscale(k):
    if not WIDE:
        return np.ones(k)
    levels = np.array([10, -10, 5, -5, 0])
    if k % 512:
        return np.exp2(np.random.permutation(np.resize(levels, k // 32))).repeat(32)
    a = np.empty((k // 512, 16))
    for p in range(k // 512):
        a[p, :8] = np.random.permutation(np.resize(levels, 8))
        for g in range(8):
            far = levels[np.abs(levels - a[p, g]) >= 10]
            a[p, g + 8] = far[np.random.randint(len(far))]
    return np.exp2(a.ravel()).repeat(32)


BF16 = ml_dtypes.bfloat16


def bf(x):
    return np.asarray(x, np.float32).astype(BF16)


def f64(x):
    return np.asarray(x).astype(np.float64)


M, S, G = 4096, 512, 1024


def draw0():
    s, v = mx_kscale(S), mx_kscale(S)
    u = mx_kscale(M)
    d = np.random.standard_normal((S, S)) / np.sqrt(S)
    d = d - d.mean(axis=0)
    p = np.random.standard_normal((S, S)) ** 4
    p = p / p.sum(axis=0)
    return {"left": bf(np.random.standard_normal((M, S)) ** 2 * s),
            "right": bf(np.random.standard_normal((M, S)) ** 2 * v),
            "d_left": bf(d / s[:, None]),
            "p_right": bf(p / v[:, None]),
            "rescale": bf(np.random.uniform(0.5, 1.5, M) * u),
            "load": bf(np.random.standard_normal((G, M)) / np.sqrt(M) / u),
            "freq": bf(np.random.uniform(0.5, 1.5, S))}


def core(left, right, d_left, p_right, rescale, load, freq):
    a = mxq(f64(left), 1, "e4m3") @ mxq(f64(d_left), 0, "e4m3")
    b = mxq(f64(right), 1, "e4m3") @ mxq(f64(p_right), 0, "e4m3")
    h = a * b * f64(rescale)[:, None]
    score = mxq(f64(load), 1, "e4m3") @ mxq(h, 0, "e4m3")
    return score * f64(freq)[None, :]


def e4m3fn_bytes(y):
    return np.clip(np.asarray(y, np.float64), -448.0, 448.0).astype(np.float32).astype(ml_dtypes.float8_e4m3fn).view(np.uint8)


def e4m3fn_values(b):
    return np.asarray(b, np.uint8).view(ml_dtypes.float8_e4m3fn).astype(np.float64)


def setup_inputs():
    d = draw0()
    x0 = np.asarray(d['load']).astype(np.float64)
    s = (np.max(np.abs(x0), axis=(0,), keepdims=True) / 448.0).astype(np.float32)
    out = {}
    for k, v in d.items():
        if k == 'load':
            out['load_bytes'] = e4m3fn_bytes(x0 / s.astype(np.float64))
            out['load_scale'] = s
        else:
            out[k] = v
    return out


def reference(left, right, d_left, p_right, rescale, load_bytes, load_scale, freq):
    return core(left, right, d_left, p_right, rescale, e4m3fn_values(load_bytes) * load_scale.astype(np.float64), freq)

@@ -1,0 +1,288 @@
+from contextlib import ExitStack
+
+import concourse.mybir as mybir
+from concourse.masks import make_identity
+
+M, S, G = 4096, 512, 1024
+FLOPS = 2 * (2 * M * S * S) + 2 * G * M * S
+
+F32 = mybir.dt.float32
+BF16 = mybir.dt.bfloat16
+U32 = mybir.dt.uint32
+U8 = mybir.dt.uint8
+FP8 = mybir.dt.float8_e4m3fn
+FP8X4 = mybir.dt.float8_e4m3fn_x4
+COPY = mybir.ActivationFunctionType.Copy
+MULT = mybir.AluOpType.mult
+
+P = 128
+PACK = 4
+KP = P * PACK
+NG = M // KP
+NI = G // P
+CH = 1024
+NCH = M // CH
+
+
+def tile_phylo_branch_score_s7_kernel(
+    tc, left, right, d_left, p_right, rescale, load_bytes, load_scale, freq, out
+):
+    nc = tc.nc
+    with ExitStack() as ctx:
+        keep = ctx.enter_context(tc.tile_pool(name="keep", bufs=1))
+        raws = ctx.enter_context(tc.tile_pool(name="raws", bufs=3))
+        work = ctx.enter_context(tc.tile_pool(name="work", bufs=2))
+        wides = ctx.enter_context(tc.tile_pool(name="wides", bufs=4))
+        outs = ctx.enter_context(tc.tile_pool(name="outs", bufs=3))
+        ps_t = ctx.enter_context(tc.psum_pool(name="ps_t", bufs=3))
+        ps_a = ctx.enter_context(tc.psum_pool(name="ps_a", bufs=3))
+        ps_b = ctx.enter_context(tc.psum_pool(name="ps_b", bufs=2))
+
+        ident = keep.tile([P, P], F32, name="ident")
+        make_identity(nc, ident[:])
+        resc_bf = keep.tile([P, NG, PACK], BF16, name="resc_bf")
+        resc = keep.tile([P, NG * PACK], F32, name="resc")
+        freq_b = keep.tile([P, S], BF16, name="freq_b")
+        scale_b = keep.tile([P, M], F32, name="scale_b")
+        mats_codes = keep.tile([P, 2, S], U32, name="mats_codes", align_bytes=64)
+        mats_scales = keep.tile([P, 2, S], U8, name="mats_scales", align_bytes=64)
+        h_codes = keep.tile([P, NG, S], U32, name="h_codes", align_bytes=64)
+        h_scales = keep.tile([P, NG, S], U8, name="h_scales", align_bytes=64)
+        bytes_t = [keep.tile([P, M], U8, name="bytes_%d" % i) for i in range(NI)]
+        warm = keep.tile([P, 1], F32, name="warm")
+
+        children = (left, right)
+        mats = (d_left, p_right)
+        raw_child = {}
+        grp_child = {}
+        codes = {}
+        scales = {}
+
+        def load_mat(s):
+            t = raws.tile([P, PACK, S], BF16, name="raw_mat%d" % s, tag="raw%d" % s, align_bytes=64)
+            nc.sync.dma_start(out=t[:], in_=mats[s].rearrange("(p j) n -> p j n", j=PACK))
+            raw_child["mat", s] = t
+
+        def load_child(s, g):
+            t = raws.tile([P, PACK, S], BF16, name="raw_%d_%d" % (s, g), tag="raw%d" % s, align_bytes=64)
+            src = children[s].rearrange("(g p t) k -> g p t k", p=P, t=PACK)
+            nc.sync.dma_start(out=t[:], in_=src[g])
+            raw_child[s, g] = t
+
+        def load_scale_chunk(c):
+            src = load_scale.rearrange("o k -> (o k)")[c * CH : (c + 1) * CH]
+            nc.sync.dma_start(out=scale_b[:, c * CH : (c + 1) * CH], in_=src.partition_broadcast(P))
+
+        def load_bytes_tile(i):
+            nc.sync.dma_start(out=bytes_t[i][:], in_=load_bytes[i * P : (i + 1) * P, :])
+
+        def mat_interleave(s):
+            t = work.tile([P, S, PACK], BF16, name="grp_mat%d" % s, tag="grp%d" % s, align_bytes=64)
+            nc.vector.tensor_copy(out=t[:], in_=raw_child["mat", s][:].rearrange("p j n -> p n j"))
+            grp_child["mat", s] = t
+
+        def mat_quantize(s):
+            nc.vector.quantize_mx(
+                out=mats_codes[:, s, :].bitcast(FP8X4),
+                scales=mats_scales[:, s, :],
+                in_=grp_child["mat", s][:].rearrange("p n j -> p (n j)"),
+            )
+
+        def child_transpose(s, g):
+            raw = raw_child[s, g]
+            grp = work.tile([P, KP * PACK], BF16, name="grp_%d_%d" % (s, g), tag="grp%d" % s, align_bytes=64)
+            for b in range(2):
+                ps = ps_t.tile([P, 2, 2, P], F32, name="tr_%d_%d_%d" % (s, g, b), tag="tr")
+                for tt in range(2):
+                    words = raw[:, 2 * b + tt, :].bitcast(F32)
+                    for u in range(2):
+                        nc.tensor.transpose(ps[:, tt, u, :], words[:, u::2], ident[:])
+                dst = grp[:].bitcast(F32)[:, b * 512 : (b + 1) * 512]
+                nc.scalar.copy(
+                    out=dst.rearrange("p (t r u) -> p t r u", t=2, u=2),
+                    in_=ps[:].rearrange("p t u r -> p t r u"),
+                )
+            grp_child[s, g] = grp
+
+        def child_quantize(s, g):
+            cd = work.tile([P, KP], U32, name="codes_%d_%d" % (s, g), tag="codes%d" % s, align_bytes=64)
+            sc = work.tile([P, KP], U8, name="scales_%d_%d" % (s, g), tag="scales%d" % s, align_bytes=64)
+            nc.vector.quantize_mx(out=cd[:].bitcast(FP8X4), scales=sc[:], in_=grp_child[s, g][:])
+            codes[s, g] = cd
+            scales[s, g] = sc
+
+        def mm(ps, cd, sc, lo, rhs_c, rhs_s, start=True, stop=True):
+            nc.tensor.matmul_mx(
+                out=ps,
+                lhsT=cd[:, lo : lo + P].bitcast(FP8X4),
+                lhsT_scale=sc[:, lo : lo + P],
+                rhs=rhs_c.bitcast(FP8X4),
+                rhs_scale=rhs_s,
+                start=start,
+                stop=stop,
+            )
+
+        a_tiles = {}
+
+        def make_a(g):
+            a = work.tile([P, PACK, S], F32, name="a_%d" % g, tag="a", align_bytes=64)
+            for t in range(PACK):
+                ps = ps_a.tile([P, S], F32, name="psa_%d_%d" % (g, t), tag="acc")
+                mm(ps[:], codes[0, g], scales[0, g], t * P, mats_codes[:, 0, :], mats_scales[:, 0, :])
+                nc.scalar.activation(
+                    out=a[:, t, :], in_=ps[:], func=COPY, scale=resc[:, g * PACK + t : g * PACK + t + 1]
+                )
+            a_tiles[g] = a
+
+        h_tiles = {}
+
+        def make_h(g):
+            h = work.tile([P, S, PACK], BF16, name="h_%d" % g, tag="h", align_bytes=64)
+            for n in range(S // P):
+                cols = slice(n * P, (n + 1) * P)
+                ps = ps_b.tile([P, PACK, P], F32, name="psb_%d_%d" % (g, n), tag="b")
+                for t in range(PACK):
+                    mm(ps[:, t, :], codes[1, g], scales[1, g], t * P, mats_codes[:, 1, cols], mats_scales[:, 1, cols])
+                nc.vector.tensor_tensor(
+                    out=h[:, cols, :],
+                    in0=ps[:].rearrange("p t n -> p n t"),
+                    in1=a_tiles[g][:, :, cols].rearrange("p t n -> p n t"),
+                    op=MULT,
+                )
+            h_tiles[g] = h
+
+        def h_quantize(g):
+            nc.vector.quantize_mx(
+                out=h_codes[:, g, :].bitcast(FP8X4),
+                scales=h_scales[:, g, :],
+                in_=h_tiles[g][:].rearrange("p n t -> p (n t)"),
+            )
+
+        wide = {}
+
+        def widen(i, lo, hi):
+            if lo == 0:
+                wide[i] = wides.tile([P, M], BF16, name="wide_%d" % i, tag="wide", align_bytes=64)
+            cols = slice(lo, hi)
+            nc.vector.tensor_tensor(
+                out=wide[i][:, cols], in0=bytes_t[i][:, cols].bitcast(FP8), in1=scale_b[:, cols], op=MULT
+            )
+
+        grp_load = {}
+
+        def load_transpose(i, half):
+            if half == 0:
+                grp_load[i] = work.tile([P, NG * P * PACK], BF16, name="grpl_%d" % i, tag="grpl", align_bytes=64)
+            words = wide[i][:].bitcast(F32)
+            for b in range(2 * half, 2 * half + 2):
+                if b % 2 == 0:
+                    ps = ps_t.tile([P, 2, 2, P], F32, name="trl_%d_%d" % (i, b), tag="tr")
+                else:
+                    ps = ps_b.tile([P, 2, 2, P], F32, name="trl_%d_%d" % (i, b), tag="b")
+                for gg in range(2):
+                    lo = (2 * b + gg) * 2 * P
+                    for u in range(2):
+                        nc.tensor.transpose(ps[:, gg, u, :], words[:, lo + u : lo + 2 * P : 2], ident[:])
+                dst = grp_load[i][:].bitcast(F32)[:, b * 512 : (b + 1) * 512]
+                nc.scalar.copy(
+                    out=dst.rearrange("p (g r u) -> p g r u", g=2, u=2),
+                    in_=ps[:].rearrange("p g u r -> p g r u"),
+                )
+
+        def load_quantize(i, half):
+            if half == 0:
+                codes["l", i] = work.tile([P, NG * P], U32, name="codesl_%d" % i, tag="codesl", align_bytes=64)
+                scales["l", i] = work.tile([P, NG * P], U8, name="scalesl_%d" % i, tag="scalesl", align_bytes=64)
+            cols = slice(half * 512, (half + 1) * 512)
+            nc.vector.quantize_mx(
+                out=codes["l", i][:, cols].bitcast(FP8X4),
+                scales=scales["l", i][:, cols],
+                in_=grp_load[i][:, half * 2048 : (half + 1) * 2048],
+            )
+
+        acc = {}
+
+        def make_c(i):
+            ps = ps_a.tile([P, S], F32, name="psc_%d" % i, tag="acc")
+            for g in range(NG):
+                mm(ps[:], codes["l", i], scales["l", i], g * P, h_codes[:, g, :], h_scales[:, g, :],
+                   start=(g == 0), stop=(g == NG - 1))
+            acc[i] = ps
+
+        def finish(i):
+            res = outs.tile([P, S], F32, name="res_%d" % i, tag="res")
+            nc.vector.tensor_tensor(out=res[:], in0=acc[i][:], in1=freq_b[:], op=MULT)
+            nc.sync.dma_start(out=out[i * P : (i + 1) * P, :], in_=res[:])
+
+        nc.scalar.dma_start(out=resc_bf[:], in_=rescale.rearrange("(g p t) -> p g t", p=P, t=PACK))
+        nc.gpsimd.tensor_copy(out=resc[:], in_=resc_bf[:].rearrange("p g t -> p (g t)"))
+        nc.gpsimd.memset(warm[:], 0.0)
+        nc.scalar.activation(out=warm[:], in_=warm[:], func=COPY, scale=1.0)
+
+        load_mat(0)
+        load_child(0, 0)
+        load_mat(1)
+        load_child(1, 0)
+        load_scale_chunk(0)
+        load_bytes_tile(0)
+        load_child(0, 1)
+        load_child(1, 1)
+        for c in range(1, NCH):
+            load_scale_chunk(c)
+
+        with tc.manual_schedule():
+            parts = [(i, c * CH, (c + 1) * CH) for i in range(2) for c in range(NCH)]
+            parts += [(i, c * 2 * CH, (c + 1) * 2 * CH) for i in range(2, NI) for c in range(2)]
+
+            def widen_next(n):
+                for j in range(n):
+                    if parts:
+                        widen(*parts[0])
+                        parts.remove(parts[0])
+
+            mat_interleave(0)
+            child_transpose(0, 0)
+            mat_interleave(1)
+            mat_quantize(0)
+            child_quantize(0, 0)
+            child_transpose(1, 0)
+            mat_quantize(1)
+            child_quantize(1, 0)
+            widen_next(1)
+            for g in range(NG):
+                if g + 2 < NG:
+                    load_child(0, g + 2)
+                    load_child(1, g + 2)
+                if g == 0:
+                    nc.sync.dma_start(out=freq_b[:], in_=freq.partition_broadcast(P))
+                if g + 1 < NI:
+                    load_bytes_tile(g + 1)
+                make_a(g)
+                if g + 1 < NG:
+                    child_transpose(0, g + 1)
+                    child_quantize(0, g + 1)
+                    child_transpose(1, g + 1)
+                else:
+                    load_transpose(0, 0)
+                    load_quantize(0, 0)
+                    load_transpose(0, 1)
+                make_h(g)
+                if g + 1 < NG:
+                    child_quantize(1, g + 1)
+                else:
+                    load_quantize(0, 1)
+                widen_next(1)
+                h_quantize(g)
+            for i in range(NI):
+                widen_next(1)
+                if i + 1 < NI:
+                    load_transpose(i + 1, 0)
+                    load_quantize(i + 1, 0)
+                if i > 0:
+                    finish(i - 1)
+                if i + 1 < NI:
+                    load_transpose(i + 1, 1)
+                    load_quantize(i + 1, 1)
+                widen_next(1)
+                make_c(i)
+            finish(NI - 1)

@@ -35,8 +35,7 @@ def tile_phylo_branch_score_s7_kernel(
         wides = ctx.enter_context(tc.tile_pool(name="wides", bufs=4))
         outs = ctx.enter_context(tc.tile_pool(name="outs", bufs=3))
         ps_t = ctx.enter_context(tc.psum_pool(name="ps_t", bufs=3))
-        ps_a = ctx.enter_context(tc.psum_pool(name="ps_a", bufs=3))
-        ps_b = ctx.enter_context(tc.psum_pool(name="ps_b", bufs=2))
+        ps_a = ctx.enter_context(tc.psum_pool(name="ps_a", bufs=5))
 
         ident = keep.tile([P, P], F32, name="ident")
         make_identity(nc, ident[:])
@@ -58,28 +57,43 @@ def tile_phylo_branch_score_s7_kernel(
         codes = {}
         scales = {}
 
-        def load_mat(s):
-            t = raws.tile([P, PACK, S], BF16, name="raw_mat%d" % s, tag="raw%d" % s, align_bytes=64)
-            nc.sync.dma_start(out=t[:], in_=mats[s].rearrange("(p j) n -> p j n", j=PACK))
-            raw_child["mat", s] = t
+        def load_mat(s, half):
+            if half == 0:
+                raw_child["mat", s] = raws.tile(
+                    [P, 2, PACK, S // 2], BF16, name="raw_mat%d" % s, tag="raw%d" % s, align_bytes=64
+                )
+            cols = slice(half * 256, (half + 1) * 256)
+            nc.sync.dma_start(
+                out=raw_child["mat", s][:, half], in_=mats[s].rearrange("(p j) n -> p j n", j=PACK)[:, :, cols]
+            )
 
         def load_child(s, g):
             t = raws.tile([P, PACK, S], BF16, name="raw_%d_%d" % (s, g), tag="raw%d" % s, align_bytes=64)
             src = children[s].rearrange("(g p t) k -> g p t k", p=P, t=PACK)
-            nc.sync.dma_start(out=t[:], in_=src[g])
+            if g == 0:
+                for hf in (slice(0, 2), slice(2, 4)):
+                    nc.sync.dma_start(out=t[:, hf, :], in_=src[g][:, hf, :])
+            else:
+                nc.sync.dma_start(out=t[:], in_=src[g])
             raw_child[s, g] = t
 
         def load_scale_chunk(c):
             src = load_scale.rearrange("o k -> (o k)")[c * CH : (c + 1) * CH]
             nc.sync.dma_start(out=scale_b[:, c * CH : (c + 1) * CH], in_=src.partition_broadcast(P))
 
-        def load_bytes_tile(i):
-            nc.sync.dma_start(out=bytes_t[i][:], in_=load_bytes[i * P : (i + 1) * P, :])
+        def load_bytes_tile(i, lo=0, hi=M):
+            nc.sync.dma_start(out=bytes_t[i][:, lo:hi], in_=load_bytes[i * P : (i + 1) * P, lo:hi])
 
-        def mat_interleave(s):
-            t = work.tile([P, S, PACK], BF16, name="grp_mat%d" % s, tag="grp%d" % s, align_bytes=64)
-            nc.vector.tensor_copy(out=t[:], in_=raw_child["mat", s][:].rearrange("p j n -> p n j"))
-            grp_child["mat", s] = t
+        def mat_interleave(s, half):
+            if half == 0:
+                grp_child["mat", s] = work.tile(
+                    [P, S, PACK], BF16, name="grp_mat%d" % s, tag="grp%d" % s, align_bytes=64
+                )
+            cols = slice(half * 256, (half + 1) * 256)
+            nc.vector.tensor_copy(
+                out=grp_child["mat", s][:, cols, :].rearrange("p (c i) j -> p c j i", i=4),
+                in_=raw_child["mat", s][:, half].rearrange("p j (c i) -> p c j i", i=4),
+            )
 
         def mat_quantize(s):
             nc.vector.quantize_mx(
@@ -140,13 +154,13 @@ def tile_phylo_branch_score_s7_kernel(
             h = work.tile([P, S, PACK], BF16, name="h_%d" % g, tag="h", align_bytes=64)
             for n in range(S // P):
                 cols = slice(n * P, (n + 1) * P)
-                ps = ps_b.tile([P, PACK, P], F32, name="psb_%d_%d" % (g, n), tag="b")
+                ps = ps_a.tile([P, PACK, P], F32, name="psb_%d_%d" % (g, n), tag="acc")
                 for t in range(PACK):
                     mm(ps[:, t, :], codes[1, g], scales[1, g], t * P, mats_codes[:, 1, cols], mats_scales[:, 1, cols])
                 nc.vector.tensor_tensor(
-                    out=h[:, cols, :],
-                    in0=ps[:].rearrange("p t n -> p n t"),
-                    in1=a_tiles[g][:, :, cols].rearrange("p t n -> p n t"),
+                    out=h[:, cols, :].rearrange("p (c i) t -> p c t i", i=4),
+                    in0=ps[:].rearrange("p t (c i) -> p c t i", i=4),
+                    in1=a_tiles[g][:, :, cols].rearrange("p t (c i) -> p c t i", i=4),
                     op=MULT,
                 )
             h_tiles[g] = h
@@ -160,8 +174,11 @@ def tile_phylo_branch_score_s7_kernel(
 
         wide = {}
 
-        def widen(i, lo, hi):
-            if lo == 0:
+        def widen(h, lo=0, hi=2048):
+            i = h // 2
+            lo += (h % 2) * 2048
+            hi += (h % 2) * 2048
+            if i not in wide:
                 wide[i] = wides.tile([P, M], BF16, name="wide_%d" % i, tag="wide", align_bytes=64)
             cols = slice(lo, hi)
             nc.vector.tensor_tensor(
@@ -170,7 +187,8 @@ def tile_phylo_branch_score_s7_kernel(
 
         grp_load = {}
 
-        def load_transpose(i, half):
+        def load_transpose(h):
+            i, half = divmod(h, 2)
             if half == 0:
                 grp_load[i] = work.tile([P, NG * P * PACK], BF16, name="grpl_%d" % i, tag="grpl", align_bytes=64)
             words = wide[i][:].bitcast(F32)
@@ -178,7 +196,7 @@ def tile_phylo_branch_score_s7_kernel(
                 if b % 2 == 0:
                     ps = ps_t.tile([P, 2, 2, P], F32, name="trl_%d_%d" % (i, b), tag="tr")
                 else:
-                    ps = ps_b.tile([P, 2, 2, P], F32, name="trl_%d_%d" % (i, b), tag="b")
+                    ps = ps_a.tile([P, 2, 2, P], F32, name="trl_%d_%d" % (i, b), tag="acc")
                 for gg in range(2):
                     lo = (2 * b + gg) * 2 * P
                     for u in range(2):
@@ -189,7 +207,8 @@ def tile_phylo_branch_score_s7_kernel(
                     in_=ps[:].rearrange("p g u r -> p g r u"),
                 )
 
-        def load_quantize(i, half):
+        def load_quantize(h):
+            i, half = divmod(h, 2)
             if half == 0:
                 codes["l", i] = work.tile([P, NG * P], U32, name="codesl_%d" % i, tag="codesl", align_bytes=64)
                 scales["l", i] = work.tile([P, NG * P], U8, name="scalesl_%d" % i, tag="scalesl", align_bytes=64)
@@ -203,36 +222,50 @@ def tile_phylo_branch_score_s7_kernel(
         acc = {}
 
         def make_c(i):
-            ps = ps_a.tile([P, S], F32, name="psc_%d" % i, tag="acc")
-            for g in range(NG):
-                mm(ps[:], codes["l", i], scales["l", i], g * P, h_codes[:, g, :], h_scales[:, g, :],
-                   start=(g == 0), stop=(g == NG - 1))
-            acc[i] = ps
+            parts = 2 if i == NI - 1 else 1
+            w = S // parts
+            acc[i] = [ps_a.tile([P, S], F32, name="psc_%d_%d" % (i, j), tag="acc") for j in range(parts)]
+            for j in range(parts):
+                cols = slice(j * w, (j + 1) * w)
+                for g in range(NG):
+                    mm(acc[i][j][:, :w], codes["l", i], scales["l", i], g * P, h_codes[:, g, cols],
+                       h_scales[:, g, cols], start=(g == 0), stop=(g == NG - 1))
 
         def finish(i):
             res = outs.tile([P, S], F32, name="res_%d" % i, tag="res")
-            nc.vector.tensor_tensor(out=res[:], in0=acc[i][:], in1=freq_b[:], op=MULT)
-            nc.sync.dma_start(out=out[i * P : (i + 1) * P, :], in_=res[:])
+            w = S // len(acc[i])
+            for j in range(len(acc[i])):
+                cols = slice(j * w, (j + 1) * w)
+                nc.vector.tensor_tensor(out=res[:, cols], in0=acc[i][j][:, :w], in1=freq_b[:, cols], op=MULT)
+                nc.sync.dma_start(out=out[i * P : (i + 1) * P, cols], in_=res[:, cols])
 
         nc.scalar.dma_start(out=resc_bf[:], in_=rescale.rearrange("(g p t) -> p g t", p=P, t=PACK))
         nc.gpsimd.tensor_copy(out=resc[:], in_=resc_bf[:].rearrange("p g t -> p (g t)"))
         nc.gpsimd.memset(warm[:], 0.0)
         nc.scalar.activation(out=warm[:], in_=warm[:], func=COPY, scale=1.0)
 
-        load_mat(0)
+        load_mat(0, 0)
+        load_mat(0, 1)
         load_child(0, 0)
-        load_mat(1)
-        load_child(1, 0)
+        load_mat(1, 0)
+        load_mat(1, 1)
+        load_bytes_tile(0, 0, CH)
         load_scale_chunk(0)
-        load_bytes_tile(0)
+        load_bytes_tile(1, 0, CH)
+        load_child(1, 0)
         load_child(0, 1)
         load_child(1, 1)
-        for c in range(1, NCH):
+        load_scale_chunk(1)
+        load_bytes_tile(0, CH, M)
+        load_bytes_tile(1, CH, M)
+        load_child(0, 2)
+        load_child(1, 2)
+        for c in range(2, NCH):
             load_scale_chunk(c)
 
         with tc.manual_schedule():
-            parts = [(i, c * CH, (c + 1) * CH) for i in range(2) for c in range(NCH)]
-            parts += [(i, c * 2 * CH, (c + 1) * 2 * CH) for i in range(2, NI) for c in range(2)]
+            parts = [(2 * i + c // 2, c % 2 * CH, c % 2 * CH + CH) for c in range(NCH) for i in range(2)]
+            parts += [(h, 0, 2048) for h in range(4, 2 * NI)]
 
             def widen_next(n):
                 for j in range(n):
@@ -240,49 +273,63 @@ def tile_phylo_branch_score_s7_kernel(
                         widen(*parts[0])
                         parts.remove(parts[0])
 
-            mat_interleave(0)
+            mat_interleave(0, 0)
+            mat_interleave(0, 1)
             child_transpose(0, 0)
-            mat_interleave(1)
             mat_quantize(0)
-            child_quantize(0, 0)
-            child_transpose(1, 0)
+            mat_interleave(1, 0)
+            mat_interleave(1, 1)
             mat_quantize(1)
+            child_quantize(0, 0)
+            widen_next(2)
+            make_a(0)
+            child_transpose(1, 0)
             child_quantize(1, 0)
-            widen_next(1)
+            child_transpose(0, 1)
+            child_transpose(1, 1)
+            widen_next(0)
             for g in range(NG):
-                if g + 2 < NG:
-                    load_child(0, g + 2)
-                    load_child(1, g + 2)
+                if g + 3 < NG:
+                    load_child(0, g + 3)
+                    load_child(1, g + 3)
                 if g == 0:
                     nc.sync.dma_start(out=freq_b[:], in_=freq.partition_broadcast(P))
-                if g + 1 < NI:
+                if 1 <= g and g + 1 < NI:
                     load_bytes_tile(g + 1)
-                make_a(g)
+                if g > 0:
+                    make_a(g)
                 if g + 1 < NG:
-                    child_transpose(0, g + 1)
                     child_quantize(0, g + 1)
-                    child_transpose(1, g + 1)
-                else:
-                    load_transpose(0, 0)
-                    load_quantize(0, 0)
-                    load_transpose(0, 1)
-                make_h(g)
+                if g > 0:
+                    h_quantize(g - 1)
                 if g + 1 < NG:
                     child_quantize(1, g + 1)
+                if g + 2 < NG:
+                    child_transpose(0, g + 2)
+                    child_transpose(1, g + 2)
+                elif g + 2 == NG:
+                    load_transpose(0)
+                    load_transpose(1)
                 else:
-                    load_quantize(0, 1)
-                widen_next(1)
-                h_quantize(g)
+                    load_quantize(0)
+                    load_quantize(1)
+                    pass
+                widen_next((2, 1, 1, 1, 1, 1, 0, 0)[g])
+                make_h(g)
+            h_quantize(NG - 1)
             for i in range(NI):
-                widen_next(1)
+                widen_next((1, 1, 1, 1, 1, 1, 1, 0)[i])
                 if i + 1 < NI:
-                    load_transpose(i + 1, 0)
-                    load_quantize(i + 1, 0)
+                    load_transpose(2 * i + 2)
+                    load_quantize(2 * i + 2)
+                if i == NI - 2:
+                    make_c(i)
                 if i > 0:
                     finish(i - 1)
+                widen_next((1, 1, 0, 1, 1, 0, 1, 0)[i])
                 if i + 1 < NI:
-                    load_transpose(i + 1, 1)
-                    load_quantize(i + 1, 1)
-                widen_next(1)
-                make_c(i)
+                    load_transpose(2 * i + 3)
+                    load_quantize(2 * i + 3)
+                if i != NI - 2:
+                    make_c(i)
             finish(NI - 1)

@@ -221,13 +221,14 @@ def tile_phylo_branch_score_s7_kernel(
 
         acc = {}
 
-        def make_c(i):
+        def make_c(i, g_lo=0, g_hi=NG):
             parts = 2 if i == NI - 1 else 1
             w = S // parts
-            acc[i] = [ps_a.tile([P, S], F32, name="psc_%d_%d" % (i, j), tag="acc") for j in range(parts)]
+            if g_lo == 0:
+                acc[i] = [ps_a.tile([P, S], F32, name="psc_%d_%d" % (i, j), tag="acc") for j in range(parts)]
             for j in range(parts):
                 cols = slice(j * w, (j + 1) * w)
-                for g in range(NG):
+                for g in range(g_lo, g_hi):
                     mm(acc[i][j][:, :w], codes["l", i], scales["l", i], g * P, h_codes[:, g, cols],
                        h_scales[:, g, cols], start=(g == 0), stop=(g == NG - 1))
 
@@ -306,30 +307,33 @@ def tile_phylo_branch_score_s7_kernel(
                     child_quantize(1, g + 1)
                 if g + 2 < NG:
                     child_transpose(0, g + 2)
-                    child_transpose(1, g + 2)
                 elif g + 2 == NG:
                     load_transpose(0)
-                    load_transpose(1)
                 else:
                     load_quantize(0)
                     load_quantize(1)
-                    pass
-                widen_next((2, 1, 1, 1, 1, 1, 0, 0)[g])
+                widen_next((2, 1, 1, 1, 1, 1, 1, 0)[g])
                 make_h(g)
+                if g + 2 < NG:
+                    child_transpose(1, g + 2)
+                elif g + 2 == NG:
+                    load_transpose(1)
             h_quantize(NG - 1)
             for i in range(NI):
                 widen_next((1, 1, 1, 1, 1, 1, 1, 0)[i])
                 if i + 1 < NI:
                     load_transpose(2 * i + 2)
                     load_quantize(2 * i + 2)
-                if i == NI - 2:
-                    make_c(i)
+                if i < NI - 1:
+                    make_c(i, 0, 4)
                 if i > 0:
                     finish(i - 1)
-                widen_next((1, 1, 0, 1, 1, 0, 1, 0)[i])
+                widen_next((1, 0, 1, 0, 1, 0, 1, 0)[i])
                 if i + 1 < NI:
                     load_transpose(2 * i + 3)
                     load_quantize(2 * i + 3)
-                if i != NI - 2:
+                if i < NI - 1:
+                    make_c(i, 4, NG)
+                else:
                     make_c(i)
             finish(NI - 1)

@@ -139,20 +139,22 @@ def tile_phylo_branch_score_s7_kernel(
         a_tiles = {}
 
         def make_a(g):
-            a = work.tile([P, PACK, S], F32, name="a_%d" % g, tag="a", align_bytes=64)
+            a = work.tile([P, S // 4, PACK, 4], F32, name="a_%d" % g, tag="a", align_bytes=64)
             for t in range(PACK):
                 ps = ps_a.tile([P, S], F32, name="psa_%d_%d" % (g, t), tag="acc")
                 mm(ps[:], codes[0, g], scales[0, g], t * P, mats_codes[:, 0, :], mats_scales[:, 0, :])
                 nc.scalar.activation(
-                    out=a[:, t, :], in_=ps[:], func=COPY, scale=resc[:, g * PACK + t : g * PACK + t + 1]
+                    out=a[:, :, t, :], in_=ps[:].rearrange("p (c i) -> p c i", i=4), func=COPY, scale=resc[:, g * PACK + t : g * PACK + t + 1]
                 )
             a_tiles[g] = a
 
         h_tiles = {}
 
-        def make_h(g):
-            h = work.tile([P, S, PACK], BF16, name="h_%d" % g, tag="h", align_bytes=64)
-            for n in range(S // P):
+        def make_h(g, n_range):
+            if 0 in n_range:
+                h_tiles[g] = work.tile([P, S, PACK], BF16, name="h_%d" % g, tag="h", align_bytes=64)
+            h = h_tiles[g]
+            for n in n_range:
                 cols = slice(n * P, (n + 1) * P)
                 ps = ps_a.tile([P, PACK, P], F32, name="psb_%d_%d" % (g, n), tag="acc")
                 for t in range(PACK):
@@ -160,10 +162,9 @@ def tile_phylo_branch_score_s7_kernel(
                 nc.vector.tensor_tensor(
                     out=h[:, cols, :].rearrange("p (c i) t -> p c t i", i=4),
                     in0=ps[:].rearrange("p t (c i) -> p c t i", i=4),
-                    in1=a_tiles[g][:, :, cols].rearrange("p t (c i) -> p c t i", i=4),
+                    in1=a_tiles[g][:, n * P // 4 : (n + 1) * P // 4],
                     op=MULT,
                 )
-            h_tiles[g] = h
 
         def h_quantize(g):
             nc.vector.quantize_mx(
@@ -212,12 +213,15 @@ def tile_phylo_branch_score_s7_kernel(
             if half == 0:
                 codes["l", i] = work.tile([P, NG * P], U32, name="codesl_%d" % i, tag="codesl", align_bytes=64)
                 scales["l", i] = work.tile([P, NG * P], U8, name="scalesl_%d" % i, tag="scalesl", align_bytes=64)
-            cols = slice(half * 512, (half + 1) * 512)
-            nc.vector.quantize_mx(
-                out=codes["l", i][:, cols].bitcast(FP8X4),
-                scales=scales["l", i][:, cols],
-                in_=grp_load[i][:, half * 2048 : (half + 1) * 2048],
-            )
+            n = 2 if h == 2 * NI - 1 else 1
+            for j in range(n):
+                lo = half * 512 + j * 512 // n
+                hi = lo + 512 // n
+                nc.vector.quantize_mx(
+                    out=codes["l", i][:, lo:hi].bitcast(FP8X4),
+                    scales=scales["l", i][:, lo:hi],
+                    in_=grp_load[i][:, PACK * lo : PACK * hi],
+                )
 
         acc = {}
 
@@ -240,25 +244,26 @@ def tile_phylo_branch_score_s7_kernel(
                 nc.vector.tensor_tensor(out=res[:, cols], in0=acc[i][j][:, :w], in1=freq_b[:, cols], op=MULT)
                 nc.sync.dma_start(out=out[i * P : (i + 1) * P, cols], in_=res[:, cols])
 
-        nc.scalar.dma_start(out=resc_bf[:], in_=rescale.rearrange("(g p t) -> p g t", p=P, t=PACK))
-        nc.gpsimd.tensor_copy(out=resc[:], in_=resc_bf[:].rearrange("p g t -> p (g t)"))
         nc.gpsimd.memset(warm[:], 0.0)
         nc.scalar.activation(out=warm[:], in_=warm[:], func=COPY, scale=1.0)
-
         load_mat(0, 0)
         load_mat(0, 1)
         load_child(0, 0)
         load_mat(1, 0)
         load_mat(1, 1)
+        nc.scalar.dma_start(out=resc_bf[:], in_=rescale.rearrange("(g p t) -> p g t", p=P, t=PACK))
+        nc.gpsimd.tensor_copy(out=resc[:], in_=resc_bf[:].rearrange("p g t -> p (g t)"))
+        load_child(1, 0)
         load_bytes_tile(0, 0, CH)
         load_scale_chunk(0)
         load_bytes_tile(1, 0, CH)
-        load_child(1, 0)
         load_child(0, 1)
-        load_child(1, 1)
         load_scale_chunk(1)
-        load_bytes_tile(0, CH, M)
-        load_bytes_tile(1, CH, M)
+        load_bytes_tile(0, CH, 2 * CH)
+        load_child(1, 1)
+        load_bytes_tile(1, CH, 2 * CH)
+        load_bytes_tile(0, 2 * CH, M)
+        load_bytes_tile(1, 2 * CH, M)
         load_child(0, 2)
         load_child(1, 2)
         for c in range(2, NCH):
@@ -266,7 +271,8 @@ def tile_phylo_branch_score_s7_kernel(
 
         with tc.manual_schedule():
             parts = [(2 * i + c // 2, c % 2 * CH, c % 2 * CH + CH) for c in range(NCH) for i in range(2)]
-            parts += [(h, 0, 2048) for h in range(4, 2 * NI)]
+            parts += [(h, 0, 2048) for h in range(4, 2 * NI - 1)]
+            parts += [(2 * NI - 1, 0, CH), (2 * NI - 1, CH, 2 * CH)]
 
             def widen_next(n):
                 for j in range(n):
@@ -282,58 +288,55 @@ def tile_phylo_branch_score_s7_kernel(
             mat_interleave(1, 1)
             mat_quantize(1)
             child_quantize(0, 0)
-            widen_next(2)
-            make_a(0)
             child_transpose(1, 0)
-            child_quantize(1, 0)
-            child_transpose(0, 1)
-            child_transpose(1, 1)
-            widen_next(0)
+            widen_next(1)
             for g in range(NG):
-                if g + 3 < NG:
-                    load_child(0, g + 3)
-                    load_child(1, g + 3)
-                if g == 0:
+                if g + 2 < NG and g > 0:
+                    load_child(0, g + 2)
+                    load_child(1, g + 2)
+                if g == 1:
                     nc.sync.dma_start(out=freq_b[:], in_=freq.partition_broadcast(P))
-                if 1 <= g and g + 1 < NI:
-                    load_bytes_tile(g + 1)
-                if g > 0:
-                    make_a(g)
-                if g + 1 < NG:
-                    child_quantize(0, g + 1)
+                if g > 1:
+                    load_bytes_tile(g)
+                make_a(g)
+                child_quantize(1, g)
+                widen_next((1, 0, 0, 0, 0, 0, 0, 0)[g])
                 if g > 0:
                     h_quantize(g - 1)
                 if g + 1 < NG:
-                    child_quantize(1, g + 1)
-                if g + 2 < NG:
-                    child_transpose(0, g + 2)
-                elif g + 2 == NG:
+                    child_transpose(0, g + 1)
+                else:
                     load_transpose(0)
+                widen_next((1, 1, 1, 1, 1, 1, 1, 1)[g])
+                make_h(g, (0, 1))
+                if g + 1 < NG:
+                    child_quantize(0, g + 1)
                 else:
                     load_quantize(0)
-                    load_quantize(1)
-                widen_next((2, 1, 1, 1, 1, 1, 1, 0)[g])
-                make_h(g)
-                if g + 2 < NG:
-                    child_transpose(1, g + 2)
-                elif g + 2 == NG:
+                make_h(g, (2, 3))
+                if g + 1 < NG:
+                    child_transpose(1, g + 1)
+                else:
                     load_transpose(1)
+            load_quantize(1)
+            widen_next(0)
             h_quantize(NG - 1)
-            for i in range(NI):
-                widen_next((1, 1, 1, 1, 1, 1, 1, 0)[i])
-                if i + 1 < NI:
-                    load_transpose(2 * i + 2)
-                    load_quantize(2 * i + 2)
-                if i < NI - 1:
-                    make_c(i, 0, 4)
+            for i in range(NI - 1):
+                load_transpose(2 * i + 2)
+                widen_next((1, 1, 1, 1, 1, 1, 2)[i])
                 if i > 0:
                     finish(i - 1)
-                widen_next((1, 0, 1, 0, 1, 0, 1, 0)[i])
-                if i + 1 < NI:
-                    load_transpose(2 * i + 3)
-                    load_quantize(2 * i + 3)
-                if i < NI - 1:
+                make_c(i, 0, 4)
+                load_quantize(2 * i + 2)
+                if i == NI - 2:
                     make_c(i, 4, NG)
-                else:
-                    make_c(i)
+                load_transpose(2 * i + 3)
+                if i == NI - 2:
+                    make_c(i + 1, 0, 4)
+                    finish(i)
+                widen_next((1, 0, 1, 0, 1, 0, 0)[i])
+                load_quantize(2 * i + 3)
+                if i < NI - 2:
+                    make_c(i, 4, NG)
+            make_c(NI - 1, 4, NG)
             finish(NI - 1)

@@ -57,15 +57,10 @@ def tile_phylo_branch_score_s7_kernel(
         codes = {}
         scales = {}
 
-        def load_mat(s, half):
-            if half == 0:
-                raw_child["mat", s] = raws.tile(
-                    [P, 2, PACK, S // 2], BF16, name="raw_mat%d" % s, tag="raw%d" % s, align_bytes=64
-                )
-            cols = slice(half * 256, (half + 1) * 256)
-            nc.sync.dma_start(
-                out=raw_child["mat", s][:, half], in_=mats[s].rearrange("(p j) n -> p j n", j=PACK)[:, :, cols]
-            )
+        def load_mat(s):
+            t = raws.tile([P, PACK, S], BF16, name="raw_mat%d" % s, tag="raw%d" % s, align_bytes=64)
+            nc.sync.dma_start(out=t[:], in_=mats[s].rearrange("(p j) n -> p j n", j=PACK))
+            raw_child["mat", s] = t
 
         def load_child(s, g):
             t = raws.tile([P, PACK, S], BF16, name="raw_%d_%d" % (s, g), tag="raw%d" % s, align_bytes=64)
@@ -77,23 +72,20 @@ def tile_phylo_branch_score_s7_kernel(
                 nc.sync.dma_start(out=t[:], in_=src[g])
             raw_child[s, g] = t
 
-        def load_scale_chunk(c):
-            src = load_scale.rearrange("o k -> (o k)")[c * CH : (c + 1) * CH]
-            nc.sync.dma_start(out=scale_b[:, c * CH : (c + 1) * CH], in_=src.partition_broadcast(P))
+        def load_scale_cols(lo, hi):
+            src = load_scale.rearrange("o k -> (o k)")[lo:hi]
+            nc.sync.dma_start(out=scale_b[:, lo:hi], in_=src.partition_broadcast(P))
 
         def load_bytes_tile(i, lo=0, hi=M):
             nc.sync.dma_start(out=bytes_t[i][:, lo:hi], in_=load_bytes[i * P : (i + 1) * P, lo:hi])
 
-        def mat_interleave(s, half):
-            if half == 0:
-                grp_child["mat", s] = work.tile(
-                    [P, S, PACK], BF16, name="grp_mat%d" % s, tag="grp%d" % s, align_bytes=64
-                )
-            cols = slice(half * 256, (half + 1) * 256)
+        def mat_interleave(s):
+            t = work.tile([P, S, PACK], BF16, name="grp_mat%d" % s, tag="grp%d" % s, align_bytes=64)
             nc.vector.tensor_copy(
-                out=grp_child["mat", s][:, cols, :].rearrange("p (c i) j -> p c j i", i=4),
-                in_=raw_child["mat", s][:, half].rearrange("p j (c i) -> p c j i", i=4),
+                out=t[:].rearrange("p (c i) j -> p c j i", i=4),
+                in_=raw_child["mat", s][:].rearrange("p j (c i) -> p c j i", i=4),
             )
+            grp_child["mat", s] = t
 
         def mat_quantize(s):
             nc.vector.quantize_mx(
@@ -175,10 +167,7 @@ def tile_phylo_branch_score_s7_kernel(
 
         wide = {}
 
-        def widen(h, lo=0, hi=2048):
-            i = h // 2
-            lo += (h % 2) * 2048
-            hi += (h % 2) * 2048
+        def widen(i, lo, hi):
             if i not in wide:
                 wide[i] = wides.tile([P, M], BF16, name="wide_%d" % i, tag="wide", align_bytes=64)
             cols = slice(lo, hi)
@@ -246,33 +235,30 @@ def tile_phylo_branch_score_s7_kernel(
 
         nc.gpsimd.memset(warm[:], 0.0)
         nc.scalar.activation(out=warm[:], in_=warm[:], func=COPY, scale=1.0)
-        load_mat(0, 0)
-        load_mat(0, 1)
+        load_mat(0)
         load_child(0, 0)
-        load_mat(1, 0)
-        load_mat(1, 1)
+        load_mat(1)
         nc.scalar.dma_start(out=resc_bf[:], in_=rescale.rearrange("(g p t) -> p g t", p=P, t=PACK))
         nc.gpsimd.tensor_copy(out=resc[:], in_=resc_bf[:].rearrange("p g t -> p (g t)"))
         load_child(1, 0)
-        load_bytes_tile(0, 0, CH)
-        load_scale_chunk(0)
-        load_bytes_tile(1, 0, CH)
+        for i in (0, 1):
+            load_bytes_tile(i, 0, CH)
+        load_scale_cols(0, 512)
+        for i in (2, 3):
+            load_bytes_tile(i, 0, CH)
         load_child(0, 1)
-        load_scale_chunk(1)
-        load_bytes_tile(0, CH, 2 * CH)
+        load_scale_cols(512, CH)
         load_child(1, 1)
-        load_bytes_tile(1, CH, 2 * CH)
-        load_bytes_tile(0, 2 * CH, M)
-        load_bytes_tile(1, 2 * CH, M)
         load_child(0, 2)
         load_child(1, 2)
-        for c in range(2, NCH):
-            load_scale_chunk(c)
 
         with tc.manual_schedule():
-            parts = [(2 * i + c // 2, c % 2 * CH, c % 2 * CH + CH) for c in range(NCH) for i in range(2)]
-            parts += [(h, 0, 2048) for h in range(4, 2 * NI - 1)]
-            parts += [(2 * NI - 1, 0, CH), (2 * NI - 1, CH, 2 * CH)]
+            parts = [(i, lo, hi) for lo, hi in ((0, 512), (512, 1024), (1024, 2048)) for i in range(4)]
+            parts += [(i, lo, lo + CH) for lo in (2 * CH, 3 * CH) for i in range(2)]
+            parts += [(i, 2 * CH, M) for i in (2, 3)]
+            parts += [(i, lo, lo + 2 * CH) for i in range(4, NI) for lo in (0, 2 * CH)]
+            parts.remove((NI - 1, 2 * CH, M))
+            parts += [(NI - 1, lo, lo + CH) for lo in (2 * CH, 3 * CH)]
 
             def widen_next(n):
                 for j in range(n):
@@ -280,34 +266,40 @@ def tile_phylo_branch_score_s7_kernel(
                         widen(*parts[0])
                         parts.remove(parts[0])
 
-            mat_interleave(0, 0)
-            mat_interleave(0, 1)
+            mat_interleave(0)
             child_transpose(0, 0)
             mat_quantize(0)
-            mat_interleave(1, 0)
-            mat_interleave(1, 1)
+            mat_interleave(1)
             mat_quantize(1)
             child_quantize(0, 0)
             child_transpose(1, 0)
-            widen_next(1)
+            widen_next(2)
             for g in range(NG):
-                if g + 2 < NG and g > 0:
+                if g == 0:
+                    load_scale_cols(CH, 2 * CH)
+                    for i in range(4):
+                        load_bytes_tile(i, CH, M)
+                elif g + 2 < NG:
                     load_child(0, g + 2)
                     load_child(1, g + 2)
-                if g == 1:
+                if g == 2:
+                    load_scale_cols(2 * CH, 3 * CH)
+                if g == 3:
+                    load_scale_cols(3 * CH, M)
+                if g == 5:
                     nc.sync.dma_start(out=freq_b[:], in_=freq.partition_broadcast(P))
-                if g > 1:
+                if g >= 4:
                     load_bytes_tile(g)
                 make_a(g)
                 child_quantize(1, g)
-                widen_next((1, 0, 0, 0, 0, 0, 0, 0)[g])
+                widen_next((5, 0, 0, 0, 0, 0, 0, 0)[g])
                 if g > 0:
                     h_quantize(g - 1)
                 if g + 1 < NG:
                     child_transpose(0, g + 1)
                 else:
                     load_transpose(0)
-                widen_next((1, 1, 1, 1, 1, 1, 1, 1)[g])
+                widen_next((1, 1, 1, 1, 1, 2, 1, 1)[g])
                 make_h(g, (0, 1))
                 if g + 1 < NG:
                     child_quantize(0, g + 1)

from contextlib import ExitStack

import concourse.mybir as mybir
from concourse.masks import make_identity

M, S, G = 4096, 512, 1024
FLOPS = 2 * (2 * M * S * S) + 2 * G * M * S

F32 = mybir.dt.float32
BF16 = mybir.dt.bfloat16
U32 = mybir.dt.uint32
U8 = mybir.dt.uint8
FP8 = mybir.dt.float8_e4m3fn
FP8X4 = mybir.dt.float8_e4m3fn_x4
COPY = mybir.ActivationFunctionType.Copy
MULT = mybir.AluOpType.mult

P = 128
PACK = 4
KP = P * PACK
NG = M // KP
NI = G // P
CH = 1024
NCH = M // CH


def tile_phylo_branch_score_s7_kernel(
    tc, left, right, d_left, p_right, rescale, load_bytes, load_scale, freq, out
):
    nc = tc.nc
    with ExitStack() as ctx:
        keep = ctx.enter_context(tc.tile_pool(name="keep", bufs=1))
        raws = ctx.enter_context(tc.tile_pool(name="raws", bufs=3))
        work = ctx.enter_context(tc.tile_pool(name="work", bufs=2))
        wides = ctx.enter_context(tc.tile_pool(name="wides", bufs=4))
        outs = ctx.enter_context(tc.tile_pool(name="outs", bufs=3))
        ps_t = ctx.enter_context(tc.psum_pool(name="ps_t", bufs=3))
        ps_a = ctx.enter_context(tc.psum_pool(name="ps_a", bufs=5))

        ident = keep.tile([P, P], F32, name="ident")
        make_identity(nc, ident[:])
        resc_bf = keep.tile([P, NG, PACK], BF16, name="resc_bf")
        resc = keep.tile([P, NG * PACK], F32, name="resc")
        freq_b = keep.tile([P, S], BF16, name="freq_b")
        scale_b = keep.tile([P, M], F32, name="scale_b")
        mats_codes = keep.tile([P, 2, S], U32, name="mats_codes", align_bytes=64)
        mats_scales = keep.tile([P, 2, S], U8, name="mats_scales", align_bytes=64)
        h_codes = keep.tile([P, NG, S], U32, name="h_codes", align_bytes=64)
        h_scales = keep.tile([P, NG, S], U8, name="h_scales", align_bytes=64)
        bytes_t = [keep.tile([P, M], U8, name="bytes_%d" % i) for i in range(NI)]
        warm = keep.tile([P, 1], F32, name="warm")

        children = (left, right)
        mats = (d_left, p_right)
        raw_child = {}
        grp_child = {}
        codes = {}
        scales = {}

        def load_mat(s):
            t = raws.tile([P, PACK, S], BF16, name="raw_mat%d" % s, tag="raw%d" % s, align_bytes=64)
            nc.sync.dma_start(out=t[:], in_=mats[s].rearrange("(p j) n -> p j n", j=PACK))
            raw_child["mat", s] = t

        def load_child(s, g):
            t = raws.tile([P, PACK, S], BF16, name="raw_%d_%d" % (s, g), tag="raw%d" % s, align_bytes=64)
            src = children[s].rearrange("(g p t) k -> g p t k", p=P, t=PACK)
            if g == 0:
                for hf in (slice(0, 2), slice(2, 4)):
                    nc.sync.dma_start(out=t[:, hf, :], in_=src[g][:, hf, :])
            else:
                nc.sync.dma_start(out=t[:], in_=src[g])
            raw_child[s, g] = t

        def load_scale_cols(lo, hi):
            src = load_scale.rearrange("o k -> (o k)")[lo:hi]
            nc.sync.dma_start(out=scale_b[:, lo:hi], in_=src.partition_broadcast(P))

        def load_bytes_tile(i, lo=0, hi=M):
            nc.sync.dma_start(out=bytes_t[i][:, lo:hi], in_=load_bytes[i * P : (i + 1) * P, lo:hi])

        def mat_interleave(s):
            t = work.tile([P, S, PACK], BF16, name="grp_mat%d" % s, tag="grp%d" % s, align_bytes=64)
            nc.vector.tensor_copy(
                out=t[:].rearrange("p (c i) j -> p c j i", i=4),
                in_=raw_child["mat", s][:].rearrange("p j (c i) -> p c j i", i=4),
            )
            grp_child["mat", s] = t

        def mat_quantize(s):
            nc.vector.quantize_mx(
                out=mats_codes[:, s, :].bitcast(FP8X4),
                scales=mats_scales[:, s, :],
                in_=grp_child["mat", s][:].rearrange("p n j -> p (n j)"),
            )

        def child_transpose(s, g):
            raw = raw_child[s, g]
            grp = work.tile([P, KP * PACK], BF16, name="grp_%d_%d" % (s, g), tag="grp%d" % s, align_bytes=64)
            for b in range(2):
                ps = ps_t.tile([P, 2, 2, P], F32, name="tr_%d_%d_%d" % (s, g, b), tag="tr")
                for tt in range(2):
                    words = raw[:, 2 * b + tt, :].bitcast(F32)
                    for u in range(2):
                        nc.tensor.transpose(ps[:, tt, u, :], words[:, u::2], ident[:])
                dst = grp[:].bitcast(F32)[:, b * 512 : (b + 1) * 512]
                nc.scalar.copy(
                    out=dst.rearrange("p (t r u) -> p t r u", t=2, u=2),
                    in_=ps[:].rearrange("p t u r -> p t r u"),
                )
            grp_child[s, g] = grp

        def child_quantize(s, g):
            cd = work.tile([P, KP], U32, name="codes_%d_%d" % (s, g), tag="codes%d" % s, align_bytes=64)
            sc = work.tile([P, KP], U8, name="scales_%d_%d" % (s, g), tag="scales%d" % s, align_bytes=64)
            nc.vector.quantize_mx(out=cd[:].bitcast(FP8X4), scales=sc[:], in_=grp_child[s, g][:])
            codes[s, g] = cd
            scales[s, g] = sc

        def mm(ps, cd, sc, lo, rhs_c, rhs_s, start=True, stop=True):
            nc.tensor.matmul_mx(
                out=ps,
                lhsT=cd[:, lo : lo + P].bitcast(FP8X4),
                lhsT_scale=sc[:, lo : lo + P],
                rhs=rhs_c.bitcast(FP8X4),
                rhs_scale=rhs_s,
                start=start,
                stop=stop,
            )

        a_tiles = {}

        def make_a(g):
            a = work.tile([P, S // 4, PACK, 4], F32, name="a_%d" % g, tag="a", align_bytes=64)
            for t in range(PACK):
                ps = ps_a.tile([P, S], F32, name="psa_%d_%d" % (g, t), tag="acc")
                mm(ps[:], codes[0, g], scales[0, g], t * P, mats_codes[:, 0, :], mats_scales[:, 0, :])
                nc.scalar.activation(
                    out=a[:, :, t, :], in_=ps[:].rearrange("p (c i) -> p c i", i=4), func=COPY, scale=resc[:, g * PACK + t : g * PACK + t + 1]
                )
            a_tiles[g] = a

        h_tiles = {}

        def make_h(g, n_range):
            if 0 in n_range:
                h_tiles[g] = work.tile([P, S, PACK], BF16, name="h_%d" % g, tag="h", align_bytes=64)
            h = h_tiles[g]
            for n in n_range:
                cols = slice(n * P, (n + 1) * P)
                ps = ps_a.tile([P, PACK, P], F32, name="psb_%d_%d" % (g, n), tag="acc")
                for t in range(PACK):
                    mm(ps[:, t, :], codes[1, g], scales[1, g], t * P, mats_codes[:, 1, cols], mats_scales[:, 1, cols])
                nc.vector.tensor_tensor(
                    out=h[:, cols, :].rearrange("p (c i) t -> p c t i", i=4),
                    in0=ps[:].rearrange("p t (c i) -> p c t i", i=4),
                    in1=a_tiles[g][:, n * P // 4 : (n + 1) * P // 4],
                    op=MULT,
                )

        def h_quantize(g):
            nc.vector.quantize_mx(
                out=h_codes[:, g, :].bitcast(FP8X4),
                scales=h_scales[:, g, :],
                in_=h_tiles[g][:].rearrange("p n t -> p (n t)"),
            )

        wide = {}

        def widen(i, lo, hi):
            if i not in wide:
                wide[i] = wides.tile([P, M], BF16, name="wide_%d" % i, tag="wide", align_bytes=64)
            cols = slice(lo, hi)
            nc.vector.tensor_tensor(
                out=wide[i][:, cols], in0=bytes_t[i][:, cols].bitcast(FP8), in1=scale_b[:, cols], op=MULT
            )

        grp_load = {}

        def load_transpose(h):
            i, half = divmod(h, 2)
            if half == 0:
                grp_load[i] = work.tile([P, NG * P * PACK], BF16, name="grpl_%d" % i, tag="grpl", align_bytes=64)
            words = wide[i][:].bitcast(F32)
            for b in range(2 * half, 2 * half + 2):
                if b % 2 == 0:
                    ps = ps_t.tile([P, 2, 2, P], F32, name="trl_%d_%d" % (i, b), tag="tr")
                else:
                    ps = ps_a.tile([P, 2, 2, P], F32, name="trl_%d_%d" % (i, b), tag="acc")
                for gg in range(2):
                    lo = (2 * b + gg) * 2 * P
                    for u in range(2):
                        nc.tensor.transpose(ps[:, gg, u, :], words[:, lo + u : lo + 2 * P : 2], ident[:])
                dst = grp_load[i][:].bitcast(F32)[:, b * 512 : (b + 1) * 512]
                nc.scalar.copy(
                    out=dst.rearrange("p (g r u) -> p g r u", g=2, u=2),
                    in_=ps[:].rearrange("p g u r -> p g r u"),
                )

        def load_quantize(h):
            i, half = divmod(h, 2)
            if half == 0:
                codes["l", i] = work.tile([P, NG * P], U32, name="codesl_%d" % i, tag="codesl", align_bytes=64)
                scales["l", i] = work.tile([P, NG * P], U8, name="scalesl_%d" % i, tag="scalesl", align_bytes=64)
            n = 2 if h == 2 * NI - 1 else 1
            for j in range(n):
                lo = half * 512 + j * 512 // n
                hi = lo + 512 // n
                nc.vector.quantize_mx(
                    out=codes["l", i][:, lo:hi].bitcast(FP8X4),
                    scales=scales["l", i][:, lo:hi],
                    in_=grp_load[i][:, PACK * lo : PACK * hi],
                )

        acc = {}

        def make_c(i, g_lo=0, g_hi=NG):
            parts = 2 if i == NI - 1 else 1
            w = S // parts
            if g_lo == 0:
                acc[i] = [ps_a.tile([P, S], F32, name="psc_%d_%d" % (i, j), tag="acc") for j in range(parts)]
            for j in range(parts):
                cols = slice(j * w, (j + 1) * w)
                for g in range(g_lo, g_hi):
                    mm(acc[i][j][:, :w], codes["l", i], scales["l", i], g * P, h_codes[:, g, cols],
                       h_scales[:, g, cols], start=(g == 0), stop=(g == NG - 1))

        def finish(i):
            res = outs.tile([P, S], F32, name="res_%d" % i, tag="res")
            w = S // len(acc[i])
            for j in range(len(acc[i])):
                cols = slice(j * w, (j + 1) * w)
                nc.vector.tensor_tensor(out=res[:, cols], in0=acc[i][j][:, :w], in1=freq_b[:, cols], op=MULT)
                nc.sync.dma_start(out=out[i * P : (i + 1) * P, cols], in_=res[:, cols])

        nc.gpsimd.memset(warm[:], 0.0)
        nc.scalar.activation(out=warm[:], in_=warm[:], func=COPY, scale=1.0)
        load_mat(0)
        load_child(0, 0)
        load_mat(1)
        nc.scalar.dma_start(out=resc_bf[:], in_=rescale.rearrange("(g p t) -> p g t", p=P, t=PACK))
        nc.gpsimd.tensor_copy(out=resc[:], in_=resc_bf[:].rearrange("p g t -> p (g t)"))
        load_child(1, 0)
        for i in (0, 1):
            load_bytes_tile(i, 0, CH)
        load_scale_cols(0, 512)
        for i in (2, 3):
            load_bytes_tile(i, 0, CH)
        load_child(0, 1)
        load_scale_cols(512, CH)
        load_child(1, 1)
        load_child(0, 2)
        load_child(1, 2)

        with tc.manual_schedule():
            parts = [(i, lo, hi) for lo, hi in ((0, 512), (512, 1024), (1024, 2048)) for i in range(4)]
            parts += [(i, lo, lo + CH) for lo in (2 * CH, 3 * CH) for i in range(2)]
            parts += [(i, 2 * CH, M) for i in (2, 3)]
            parts += [(i, lo, lo + 2 * CH) for i in range(4, NI) for lo in (0, 2 * CH)]
            parts.remove((NI - 1, 2 * CH, M))
            parts += [(NI - 1, lo, lo + CH) for lo in (2 * CH, 3 * CH)]

            def widen_next(n):
                for j in range(n):
                    if parts:
                        widen(*parts[0])
                        parts.remove(parts[0])

            mat_interleave(0)
            child_transpose(0, 0)
            mat_quantize(0)
            mat_interleave(1)
            mat_quantize(1)
            child_quantize(0, 0)
            child_transpose(1, 0)
            widen_next(2)
            for g in range(NG):
                if g == 0:
                    load_scale_cols(CH, 2 * CH)
                    for i in range(4):
                        load_bytes_tile(i, CH, M)
                elif g + 2 < NG:
                    load_child(0, g + 2)
                    load_child(1, g + 2)
                if g == 2:
                    load_scale_cols(2 * CH, 3 * CH)
                if g == 3:
                    load_scale_cols(3 * CH, M)
                if g == 5:
                    nc.sync.dma_start(out=freq_b[:], in_=freq.partition_broadcast(P))
                if g >= 4:
                    load_bytes_tile(g)
                make_a(g)
                child_quantize(1, g)
                widen_next((5, 0, 0, 0, 0, 0, 0, 0)[g])
                if g > 0:
                    h_quantize(g - 1)
                if g + 1 < NG:
                    child_transpose(0, g + 1)
                else:
                    load_transpose(0)
                widen_next((1, 1, 1, 1, 1, 2, 1, 1)[g])
                make_h(g, (0, 1))
                if g + 1 < NG:
                    child_quantize(0, g + 1)
                else:
                    load_quantize(0)
                make_h(g, (2, 3))
                if g + 1 < NG:
                    child_transpose(1, g + 1)
                else:
                    load_transpose(1)
            load_quantize(1)
            widen_next(0)
            h_quantize(NG - 1)
            for i in range(NI - 1):
                load_transpose(2 * i + 2)
                widen_next((1, 1, 1, 1, 1, 1, 2)[i])
                if i > 0:
                    finish(i - 1)
                make_c(i, 0, 4)
                load_quantize(2 * i + 2)
                if i == NI - 2:
                    make_c(i, 4, NG)
                load_transpose(2 * i + 3)
                if i == NI - 2:
                    make_c(i + 1, 0, 4)
                    finish(i)
                widen_next((1, 0, 1, 0, 1, 0, 0)[i])
                load_quantize(2 * i + 3)
                if i < NI - 2:
                    make_c(i, 4, NG)
            make_c(NI - 1, 4, NG)
            finish(NI - 1)
